import numpy as np
import ml_dtypes


def mxq(x, axis, fmt="e4m3"):
    dtype, down = {"e4m3": (ml_dtypes.float8_e4m3fn, 7), "e5m2": (ml_dtypes.float8_e5m2, 14)}[fmt]
    v = np.moveaxis(np.asarray(x, np.float32).astype(ml_dtypes.bfloat16).astype(np.float64), axis, -1)
    blocks = v.reshape(v.shape[:-1] + (-1, 32))
    amax = np.abs(blocks).max(-1, keepdims=True)
    byte = np.maximum(np.where(amax > 0, np.frexp(amax)[1] - 1 + 127, 0) - down, 1)
    scale = np.exp2(byte - 127.0)
    codes = (blocks / scale).astype(np.float32).astype(dtype).astype(np.float64)
    return np.moveaxis((codes * scale).reshape(v.shape), -1, axis)


WIDE = False


def mx_kscale(k):
    if not WIDE:
        return np.ones(k)
    levels = np.array([10, -10, 5, -5, 0])
    if k % 512:
        return np.exp2(np.random.permutation(np.resize(levels, k // 32))).repeat(32)
    a = np.empty((k // 512, 16))
    for p in range(k // 512):
        a[p, :8] = np.random.permutation(np.resize(levels, 8))
        for g in range(8):
            far = levels[np.abs(levels - a[p, g]) >= 10]
            a[p, g + 8] = far[np.random.randint(len(far))]
    return np.exp2(a.ravel()).repeat(32)


def f64(x):
    return np.asarray(x).astype(np.float64)


def striped(idx):
    return np.tile(idx.reshape(-1, 16).T, (8, 1)).astype(np.uint16)


def unstriped(offs):
    return offs[:16].T.reshape(-1).astype(np.int64)


def striped8(idx):
    return np.concatenate([x.reshape(-1, 16).T for x in idx]).astype(np.uint16)


def runs(offs, k):
    lists = np.stack([offs[16 * r : 16 * r + 16].T.reshape(-1) for r in range(8)]).astype(np.int64)
    return lists[np.arange(k) % 512 // 64]


def pack_weight(w):
    k, n = w.shape
    w = f64(np.asarray(w, np.float32).astype(ml_dtypes.bfloat16)).reshape(k // 32, 32, n)
    amax = np.abs(w).max(1)
    byte = np.clip(np.where(amax > 0, np.frexp(amax)[1] - 1 + 127 - 7, 1), 1, 254)
    scaled = (w * np.exp2(127.0 - byte)[:, None, :]).reshape(k, n).astype(np.float32)
    words = np.ascontiguousarray(scaled.reshape(k // 512, 128, 4, n).transpose(0, 1, 3, 2)).astype(ml_dtypes.float8_e4m3fn).view(np.uint8)
    return words, np.ascontiguousarray(byte.astype(np.uint8).reshape(k // 512, 16, n))


def unpack_weight(words, scales):
    g, p, n, _ = words.shape
    vals = np.ascontiguousarray(words).view(ml_dtypes.float8_e4m3fn).astype(np.float64) * np.repeat(np.exp2(scales.astype(np.float64) - 127.0), 8, axis=1)[..., None]
    return vals.transpose(0, 1, 3, 2).reshape(g * 512, n)


K, T, S, G, H, W, U = 512, 1024, 256, 2048, 512, 128, 512


def setup_inputs():
    n = np.random.standard_normal
    s = mx_kscale(K)[:, None]
    packed_xT = pack_weight(n((K, T)) * s)
    packed_dT = pack_weight(n((K, G)) / s)
    perm = np.random.permutation(S)
    perm2 = np.random.permutation(U)
    return {
        "x_words": packed_xT[0],
        "x_scales": packed_xT[1],
        "d_words": packed_dT[0],
        "d_scales": packed_dT[1],
        "gs": (np.random.uniform(0.5, 1.5, (K, 1)) * s).astype(np.float32),
        "offs": striped(np.random.permutation(T)[:S]),
        "k1": striped8(np.random.randint(0, G, (8, H))),
        "two": striped(np.random.permutation(T)[:S]),
        "k2": striped8(np.random.randint(0, G, (8, H))),
        "hz": striped8(np.random.randint(0, T, (8, S))),
        "k3": striped8(np.random.randint(0, G, (8, H))),
        "n1": striped(perm[:W]),
        "n2": striped(perm[W:]),
        "n3": striped(np.random.permutation(S)),
        "k4": striped8(np.random.randint(0, G, (8, H))),
        "k5": striped8(np.random.randint(0, G, (8, H))),
        "hy": striped8(np.random.randint(0, T, (8, S))),
        "n4": striped(perm2[:S]),
        "n5": striped(perm2[S:]),
        "n6": striped(np.random.permutation(S)),
        "n7": striped(np.random.permutation(S)),
    }


def reference(x_words, x_scales, d_words, d_scales, gs, offs, k1, two, k2, hz, k3, n1, n2, n3, k4, k5, hy, n4, n5, n6, n7):
    d_k4 = unpack_weight(d_words, d_scales)[np.arange(K)[:, None], runs(k4, K)]
    d_k1 = unpack_weight(d_words, d_scales)[np.arange(K)[:, None], runs(k1, K)]
    xq = unpack_weight(x_words, x_scales)[:, unstriped(offs)]
    d_k2 = unpack_weight(d_words, d_scales)[np.arange(K)[:, None], runs(k2, K)]
    x_two = unpack_weight(x_words, x_scales)[:, unstriped(two)]
    d_k3 = unpack_weight(d_words, d_scales)[np.arange(K)[:, None], runs(k3, K)]
    x_hz = unpack_weight(x_words, x_scales)[np.arange(K)[:, None], runs(hz, K)]
    h = 0.0625 * (d_k1.T @ xq + d_k2.T @ x_two + d_k3.T @ x_hz)
    pa = h[:, unstriped(n1)]
    pb = h[:, unstriped(n2)]
    rb = np.minimum(pa, pb)
    ra = np.maximum(pa, pb)
    ua = np.zeros((H, S))
    ua[:, unstriped(n1)] = ra
    ub = ua.copy()
    ub[:, unstriped(n2)] = rb
    z = f64(gs) * (ub - ub[:, unstriped(n3)])
    d_k5 = unpack_weight(d_words, d_scales)[np.arange(K)[:, None], runs(k5, K)]
    x_hy = unpack_weight(x_words, x_scales)[np.arange(K)[:, None], runs(hy, K)]
    h2 = 0.0625 * ((d_k4.T @ mxq(z, 0, "e4m3") + d_k5.T @ x_hy))
    dn = h2 - h2[:, unstriped(n7)]
    up = np.maximum(h2, h2[:, unstriped(n6)])
    ph = np.zeros((H, U))
    ph[:, unstriped(n4)] = up
    out = ph.copy()
    out[:, unstriped(n5)] = dn
    return out

@@ -1,0 +1,289 @@
+from contextlib import ExitStack
+
+import concourse.mybir as mybir
+from concourse.masks import make_identity
+
+F32 = mybir.dt.float32
+BF16 = mybir.dt.bfloat16
+I32 = mybir.dt.int32
+U32 = mybir.dt.uint32
+U16 = mybir.dt.uint16
+U8 = mybir.dt.uint8
+FP8X4 = mybir.dt.float8_e4m3fn_x4
+ALU = mybir.AluOpType
+COPY = mybir.ActivationFunctionType.Copy
+
+P = 128
+K, T, S, G, H, W, U = 512, 1024, 256, 2048, 512, 128, 512
+PIECE = 256
+SPARE = 16
+FLOPS = 5 * 2 * K * H * S
+
+
+def tile_picked_mtthzmhorddpagdd_none_p_kernel(
+    tc, x_words, x_scales, d_words, d_scales, gs, offs, k1, two, k2, hz, k3, n1, n2, n3, k4, k5, hy, n4, n5, n6, n7, out
+):
+    nc = tc.nc
+    with ExitStack() as ctx:
+        lists = ctx.enter_context(tc.tile_pool(name="lists", bufs=1))
+        keep = ctx.enter_context(tc.tile_pool(name="keep", bufs=1))
+        psum = ctx.enter_context(tc.psum_pool(name="psum", bufs=2))
+
+        L = {}
+
+        def load_list(name, src):
+            L[name] = lists.tile(list(src.shape), U16, name="list_" + name)
+            nc.sync.dma_start(L[name][:], src)
+
+        def load_scales(name, src, width):
+            t = keep.tile([P, width], U8, name=name)
+            rows = src[0].bitcast(I32)
+            nc.sync.dma_start(t[:].bitcast(I32), rows.unsqueeze(1).to_broadcast([16, 8, width // 4]))
+            return t
+
+        def load_words(name, src, width):
+            t = keep.tile([P, width], I32, name=name)
+            nc.sync.dma_start(t[:], src[0].rearrange("p n t -> p (n t)").bitcast(I32))
+            return t
+
+        x_bytes = load_scales("x_bytes", x_scales, T)
+        load_list("offs", offs)
+        load_list("two", two)
+        load_list("hz", hz)
+        d_bytes = load_scales("d_bytes", d_scales, G)
+        load_list("k1", k1)
+        load_list("k2", k2)
+        load_list("k3", k3)
+        x_codes = load_words("x_codes", x_words, T)
+        d_codes = load_words("d_codes", d_words, G)
+        gs_sb = keep.tile([P, 4], F32, name="gs_sb")
+        nc.sync.dma_start(gs_sb[:], gs.rearrange("(p t) o -> p (t o)", t=4))
+        for name, src in (("n1", n1), ("n2", n2)):
+            load_list(name, src)
+
+        ident = keep.tile([P, P], F32, name="ident")
+        make_identity(nc, ident[:])
+
+        def offsets(name, piece):
+            return L[name][:, piece * PIECE // 16 : (piece + 1) * PIECE // 16]
+
+        scale_of = {}
+        words_of = {}
+
+        def gather_bytes(label, picks, after=""):
+            width = PIECE * len(picks)
+            got = keep.tile([P, width], U8, name="got_" + label, tag=after or "got_" + label, align_bytes=64)
+            plane = keep.tile([P, width], U8, name="plane_" + label, align_bytes=64)
+            nc.vector.memset(plane[:].bitcast(I32), 0)
+            for i, (name, piece) in enumerate(picks):
+                table = d_bytes if name.startswith("k") else x_bytes
+                nc.vector.tensor_copy(got[:, i * PIECE : (i + 1) * PIECE], table[:].indirect(offsets(name, piece)))
+                scale_of[name, piece] = plane[:, i * PIECE : (i + 1) * PIECE]
+            for a in range(4):
+                nc.sync.dma_start(plane[:].bitcast(I32)[a:P:32, :], got[:].bitcast(I32)[8 * a : P : 32, :])
+
+        def gather_words(name, piece, after=""):
+            table = d_codes if name.startswith("k") else x_codes
+            got = keep.tile([P, PIECE], U32, name="words_%s_%d" % (name, piece), tag=after or "words_%s_%d" % (name, piece), align_bytes=64)
+            nc.vector.tensor_copy(got[:], table[:].bitcast(U32).indirect(offsets(name, piece)))
+            words_of[name, piece] = got
+
+        def mx(acc, kname, b, rhs, rhs_scale, start, stop):
+            cols = slice((b % 2) * P, (b % 2 + 1) * P)
+            nc.tensor.matmul_mx(
+                out=acc,
+                lhsT=words_of[kname, b // 2][:, cols].bitcast(FP8X4),
+                lhsT_scale=scale_of[kname, b // 2][:, cols],
+                rhs=rhs.bitcast(FP8X4),
+                rhs_scale=rhs_scale,
+                start=start,
+                stop=stop,
+            )
+
+        g_ps = psum.tile([P, 4, P], F32, name="g_ps", tag="back")
+        for t in range(4):
+            nc.tensor.transpose(g_ps[:, t, :], gs_sb[:, t : t + 1].to_broadcast([P, P]), ident[:])
+        gain = keep.tile([P, 2, P, 2], F32, name="gain")
+        nc.scalar.activation(gain[:], g_ps[:].rearrange("j (u e) p -> j u p e", e=2), COPY, scale=0.0625)
+
+        h_sb, pa, pb, ra, rb, ub, neg, zt = {}, {}, {}, {}, {}, {}, {}, {}
+
+        def small(name, b):
+            return keep.tile([P, W], F32, name="%s%d" % (name, b), tag="%s%d" % (name, b), align_bytes=64)
+
+        def product1(c, terms):
+            acc = [psum.tile([P, S], F32, name="h_ps", tag="h") for i in range(2)]
+            for n, (kn, xn) in enumerate(terms):
+                for i in range(2):
+                    mx(acc[i][:], kn, 2 * c + i, words_of[xn, 0][:], scale_of[xn, 0], n == 0, n == 2)
+            return acc
+
+        def leave_product1(b, acc, copy):
+            h_sb[b] = keep.tile([P, S], F32, name="h%d" % b)
+            copy(h_sb[b][:], acc[:])
+
+        def fetch_pairs(b):
+            pa[b] = small("pa", b)
+            pb[b] = small("pb", b)
+            nc.scalar.activation(pa[b][:], h_sb[b][:].indirect(L["n1"][:]), COPY)
+            nc.scalar.activation(pb[b][:], h_sb[b][:].indirect(L["n2"][:]), COPY)
+
+        def order_pairs(b):
+            ra[b] = small("ra", b)
+            rb[b] = small("rb", b)
+            nc.vector.tensor_tensor(ra[b][:], pa[b][:], pb[b][:], ALU.max)
+            nc.vector.tensor_tensor(rb[b][:], pa[b][:], pb[b][:], ALU.min)
+
+        def put_larger(b):
+            ub[b] = keep.tile([P, S], F32, name="ub%d" % b)
+            nc.scalar.activation(ub[b][:].indirect(L["n1"][:]), ra[b][:], COPY)
+
+        def put_smaller(b):
+            nc.scalar.activation(ub[b][:].indirect(L["n2"][:]), rb[b][:], COPY)
+
+        def fetch_n3(b, jh):
+            neg[b, jh] = keep.tile([P, P], F32, name="neg%d_%d" % (b, jh))
+            nc.scalar.activation(neg[b, jh][:], ub[b][:].indirect(L["n3"][:, jh * 8 : (jh + 1) * 8]), COPY, scale=-1.0)
+
+        def turn(c, jh):
+            cols = slice(jh * P, (jh + 1) * P)
+            t1 = psum.tile([P, 2, P], F32, name="t1", tag="h" if c == 0 else "turn")
+            for i in range(2):
+                b = 2 * c + i
+                nc.tensor.matmul(t1[:, i, :], ub[b][:, cols], ident[:], start=True, stop=False, is_transpose=True)
+                nc.tensor.matmul(t1[:, i, :], neg[b, jh][:], ident[:], start=False, stop=True, is_transpose=True)
+            ps = slice(64 * c, 64 * (c + 1))
+            nc.vector.tensor_tensor(
+                zt[jh][:, :, ps, :], t1[:].rearrange("j b (q u e) -> j u (b q) e", u=2, e=2), gain[:, :, ps, :], ALU.mult
+            )
+
+        first = [("offs", 0), ("two", 0), ("hz", 0), ("k1", 0), ("k2", 0), ("k3", 0)]
+        gather_bytes("a", first)
+        for name, piece in first:
+            gather_words(name, piece)
+        for name, src in (("n3", n3), ("hy", hy), ("k4", k4), ("k5", k5)):
+            load_list(name, src)
+        acc = product1(0, (("k1", "offs"), ("k2", "two"), ("k3", "hz")))
+        leave_product1(0, acc[0], nc.scalar.copy)
+        gather_bytes("b", [("k1", 1), ("k2", 1), ("k3", 1)], "got_a")
+        for name, src in (("n6", n6), ("n7", n7), ("n4", n4), ("n5", n5)):
+            load_list(name, src)
+        fetch_pairs(0)
+        leave_product1(1, acc[1], nc.scalar.copy)
+        fetch_pairs(1)
+        order_pairs(0)
+        gather_words("k3", 1, "pa0")
+        order_pairs(1)
+        gather_words("k1", 1, "pa1")
+        gather_words("k2", 1, "pb1")
+        put_larger(0)
+        put_larger(1)
+        put_smaller(0)
+        gather_bytes("c", [("hy", 0), ("k5", 0), ("k4", 0)], "ra1")
+        put_smaller(1)
+        for jh in range(2):
+            fetch_n3(0, jh)
+        acc = product1(1, (("k3", "hz"), ("k1", "offs"), ("k2", "two")))
+        leave_product1(2, acc[0], nc.scalar.copy)
+        leave_product1(3, acc[1], nc.vector.tensor_copy)
+        fetch_pairs(2)
+        for jh in range(2):
+            fetch_n3(1, jh)
+        fetch_pairs(3)
+        gather_words("hy", 0, "pb1")
+        order_pairs(2)
+        gather_words("k5", 0, "pa2")
+        order_pairs(3)
+        gather_words("k4", 0, "pa3")
+        put_larger(2)
+        put_larger(3)
+        put_smaller(2)
+        put_smaller(3)
+        for jh, after in enumerate(("pb3", "ra2")):
+            zt[jh] = keep.tile([P, 2, P, 2], BF16, name="zt%d" % jh, tag=after, align_bytes=64)
+            turn(0, jh)
+        gather_bytes("d", [("k5", 1), ("k4", 1)], "ra3")
+        for jh in range(2):
+            fetch_n3(2, jh)
+            fetch_n3(3, jh)
+
+        o_ps = {}
+
+        def open_product2(b):
+            o_ps[b] = psum.tile([P, S], F32, name="o_ps", tag="o" if b < 2 else "h")
+            mx(o_ps[b][:], "k5", b, words_of["hy", 0][:], scale_of["hy", 0], True, False)
+
+        def close_product2(b, jh):
+            cols = slice(jh * P, (jh + 1) * P)
+            mx(o_ps[b][:, cols], "k4", b, z_codes[:, cols], z_scales[:, cols], False, jh == 1)
+
+        open_product2(0)
+        open_product2(1)
+        z_in = keep.tile([P, S, 4], BF16, name="z_in", align_bytes=64)
+        z_codes = keep.tile([P, S], U32, name="z_codes", align_bytes=64)
+        z_scales = keep.tile([P, S], U8, name="z_scales", align_bytes=64)
+        for jh in range(2):
+            turn(1, jh)
+            words = zt[jh][:].rearrange("j u p e -> j u (p e)").bitcast(F32)
+            t2 = psum.tile([P, 2, P], F32, name="t2", tag="back")
+            for u in range(2):
+                nc.tensor.transpose(t2[:, u, :], words[:, u, :], ident[:])
+            cols = slice(jh * P, (jh + 1) * P)
+            nc.scalar.copy(z_in[:, cols, :].bitcast(F32), t2[:].rearrange("p u j -> p j u"))
+            nc.vector.quantize_mx(
+                out=z_codes[:, cols].bitcast(FP8X4), scales=z_scales[:, cols], in_=z_in[:, cols, :].rearrange("p j t -> p (j t)")
+            )
+            close_product2(0, jh)
+        for jh in range(2):
+            close_product2(1, jh)
+
+        h2, got6, got7, up, dn, page = {}, {}, {}, {}, {}, {}
+
+        def leave_product2(b):
+            h2[b] = keep.tile([P, S + SPARE], F32, name="h2_%d" % b)
+            nc.gpsimd.memset(h2[b][:, S:], 0.0)
+            nc.vector.tensor_scalar(h2[b][:, :S], o_ps[b][:], 0.0625, None, ALU.mult)
+
+        def fetch2(b):
+            got6[b] = keep.tile([P, S], F32, name="got6_%d" % b, tag="got6_%d" % b, align_bytes=64)
+            got7[b] = keep.tile([P, S], F32, name="got7_%d" % b, tag="got7_%d" % b, align_bytes=64)
+            nc.scalar.activation(got6[b][:], h2[b][:].indirect(L["n6"][:]), COPY)
+            nc.scalar.activation(got7[b][:], h2[b][:].indirect(L["n7"][:]), COPY)
+
+        def combine2(b):
+            up[b] = keep.tile([P, S], F32, name="up%d" % b)
+            dn[b] = keep.tile([P, S], F32, name="dn%d" % b)
+            nc.vector.tensor_tensor(up[b][:], h2[b][:, :S], got6[b][:], ALU.max)
+            nc.vector.tensor_tensor(dn[b][:], h2[b][:, :S], got7[b][:], ALU.subtract)
+
+        def put_up(b):
+            page[b] = keep.tile([P, U], F32, name="page%d" % b)
+            nc.scalar.activation(page[b][:].indirect(L["n4"][:]), up[b][:], COPY)
+
+        def put_dn(b):
+            nc.scalar.activation(page[b][:].indirect(L["n5"][:]), dn[b][:], COPY)
+            nc.sync.dma_start(out[b * P : (b + 1) * P, :], page[b][:])
+
+        leave_product2(0)
+        fetch2(0)
+        leave_product2(1)
+        fetch2(1)
+        combine2(0)
+        gather_words("k5", 1, "got7_0")
+        combine2(1)
+        gather_words("k4", 1, "got7_1")
+        put_up(0)
+        put_up(1)
+        put_dn(0)
+        put_dn(1)
+        for b in (2, 3):
+            open_product2(b)
+            for jh in range(2):
+                close_product2(b, jh)
+            leave_product2(b)
+            fetch2(b)
+            combine2(b)
+        put_up(2)
+        put_up(3)
+        put_dn(2)
+        put_dn(3)

@@ -119,7 +119,7 @@ def tile_picked_mtthzmhorddpagdd_none_p_kernel(
             return acc
 
         def leave_product1(b, acc, copy):
-            h_sb[b] = keep.tile([P, S], F32, name="h%d" % b)
+            h_sb[b] = keep.tile([P, S], F32, name="h%d" % b, tag="h%d" % b)
             copy(h_sb[b][:], acc[:])
 
         def fetch_pairs(b):
@@ -141,18 +141,18 @@ def tile_picked_mtthzmhorddpagdd_none_p_kernel(
         def put_smaller(b):
             nc.scalar.activation(ub[b][:].indirect(L["n2"][:]), rb[b][:], COPY)
 
-        def fetch_n3(b, jh):
-            neg[b, jh] = keep.tile([P, P], F32, name="neg%d_%d" % (b, jh))
+        def fetch_n3(b, jh, after=""):
+            if (b, jh) not in neg:
+                neg[b, jh] = keep.tile([P, P], F32, name="neg%d_%d" % (b, jh))
             nc.scalar.activation(neg[b, jh][:], ub[b][:].indirect(L["n3"][:, jh * 8 : (jh + 1) * 8]), COPY, scale=-1.0)
 
-        def turn(c, jh):
+        def turn(blocks, jh, bank):
             cols = slice(jh * P, (jh + 1) * P)
-            t1 = psum.tile([P, 2, P], F32, name="t1", tag="h" if c == 0 else "turn")
-            for i in range(2):
-                b = 2 * c + i
+            t1 = psum.tile([P, len(blocks), P], F32, name="t1", tag=bank)
+            for i, b in enumerate(blocks):
                 nc.tensor.matmul(t1[:, i, :], ub[b][:, cols], ident[:], start=True, stop=False, is_transpose=True)
                 nc.tensor.matmul(t1[:, i, :], neg[b, jh][:], ident[:], start=False, stop=True, is_transpose=True)
-            ps = slice(64 * c, 64 * (c + 1))
+            ps = slice(32 * blocks[0], 32 * (blocks[-1] + 1))
             nc.vector.tensor_tensor(
                 zt[jh][:, :, ps, :], t1[:].rearrange("j b (q u e) -> j u (b q) e", u=2, e=2), gain[:, :, ps, :], ALU.mult
             )
@@ -172,58 +172,73 @@ def tile_picked_mtthzmhorddpagdd_none_p_kernel(
         leave_product1(1, acc[1], nc.scalar.copy)
         fetch_pairs(1)
         order_pairs(0)
-        gather_words("k3", 1, "pa0")
         order_pairs(1)
-        gather_words("k1", 1, "pa1")
-        gather_words("k2", 1, "pb1")
+        gather_words("k3", 1, "pa1")
+        gather_words("k1", 1, "pb1")
         put_larger(0)
         put_larger(1)
+        gather_words("k2", 1, "ra1")
         put_smaller(0)
-        gather_bytes("c", [("hy", 0), ("k5", 0), ("k4", 0)], "ra1")
+        gather_words("hy", 0, "rb0")
         put_smaller(1)
         for jh in range(2):
             fetch_n3(0, jh)
         acc = product1(1, (("k3", "hz"), ("k1", "offs"), ("k2", "two")))
-        leave_product1(2, acc[0], nc.scalar.copy)
+        leave_product1(2, acc[0], nc.vector.tensor_copy)
         leave_product1(3, acc[1], nc.vector.tensor_copy)
+        gather_bytes("c", [("hy", 0), ("k5", 0), ("k4", 0)], "ra1")
         fetch_pairs(2)
-        for jh in range(2):
-            fetch_n3(1, jh)
         fetch_pairs(3)
-        gather_words("hy", 0, "pb1")
+        late = keep.tile([P, 2, P], F32, name="neg1", tag="h2")
+        for jh in range(2):
+            neg[1, jh] = late[:, jh, :]
+            fetch_n3(1, jh)
         order_pairs(2)
-        gather_words("k5", 0, "pa2")
         order_pairs(3)
-        gather_words("k4", 0, "pa3")
+        gather_words("k5", 0, "pa3")
+        gather_words("k4", 0, "pb3")
         put_larger(2)
         put_larger(3)
         put_smaller(2)
         put_smaller(3)
-        for jh, after in enumerate(("pb3", "ra2")):
+        for jh, after in enumerate(("ra2", "ra3")):
             zt[jh] = keep.tile([P, 2, P, 2], BF16, name="zt%d" % jh, tag=after, align_bytes=64)
-            turn(0, jh)
-        gather_bytes("d", [("k5", 1), ("k4", 1)], "ra3")
+            turn((0, 1), jh, "h")
+        gather_bytes("d", [("k5", 1), ("k4", 1)], "rb2")
         for jh in range(2):
             fetch_n3(2, jh)
             fetch_n3(3, jh)
 
         o_ps = {}
 
-        def open_product2(b):
-            o_ps[b] = psum.tile([P, S], F32, name="o_ps", tag="o" if b < 2 else "h")
+        def open_product2(b, bank):
+            o_ps[b] = psum.tile([P, S], F32, name="o_ps", tag=bank)
             mx(o_ps[b][:], "k5", b, words_of["hy", 0][:], scale_of["hy", 0], True, False)
 
         def close_product2(b, jh):
             cols = slice(jh * P, (jh + 1) * P)
             mx(o_ps[b][:, cols], "k4", b, z_codes[:, cols], z_scales[:, cols], False, jh == 1)
 
-        open_product2(0)
-        open_product2(1)
+        h2 = {}
+
+        def window2(b):
+            h2[b] = keep.tile([P, S + SPARE], F32, name="h2_%d" % b)
+            nc.gpsimd.memset(h2[b][:, S:], 0.0)
+
+        half = []
+        for jh in range(2):
+            cols = slice(jh * P, (jh + 1) * P)
+            half.append(psum.tile([P, P], F32, name="o_half", tag="o"))
+            mx(half[jh][:], "k5", 0, words_of["hy", 0][:, cols], scale_of["hy", 0][:, cols], True, False)
+        window2(0)
         z_in = keep.tile([P, S, 4], BF16, name="z_in", align_bytes=64)
         z_codes = keep.tile([P, S], U32, name="z_codes", align_bytes=64)
         z_scales = keep.tile([P, S], U8, name="z_scales", align_bytes=64)
+        turn((2, 3), 0, "turn")
+        turn((2,), 1, "turn")
+        turn((3,), 1, "h")
+        open_product2(1, "h")
         for jh in range(2):
-            turn(1, jh)
             words = zt[jh][:].rearrange("j u p e -> j u (p e)").bitcast(F32)
             t2 = psum.tile([P, 2, P], F32, name="t2", tag="back")
             for u in range(2):
@@ -233,15 +248,15 @@ def tile_picked_mtthzmhorddpagdd_none_p_kernel(
             nc.vector.quantize_mx(
                 out=z_codes[:, cols].bitcast(FP8X4), scales=z_scales[:, cols], in_=z_in[:, cols, :].rearrange("p j t -> p (j t)")
             )
-            close_product2(0, jh)
+            mx(half[jh][:], "k4", 0, z_codes[:, cols], z_scales[:, cols], False, True)
+            nc.vector.tensor_scalar(h2[0][:, cols], half[jh][:], 0.0625, None, ALU.mult)
         for jh in range(2):
             close_product2(1, jh)
 
-        h2, got6, got7, up, dn, page = {}, {}, {}, {}, {}, {}
+        got6, got7, up, dn, page = {}, {}, {}, {}, {}
 
         def leave_product2(b):
-            h2[b] = keep.tile([P, S + SPARE], F32, name="h2_%d" % b)
-            nc.gpsimd.memset(h2[b][:, S:], 0.0)
+            window2(b)
             nc.vector.tensor_scalar(h2[b][:, :S], o_ps[b][:], 0.0625, None, ALU.mult)
 
         def fetch2(b):
@@ -264,7 +279,6 @@ def tile_picked_mtthzmhorddpagdd_none_p_kernel(
             nc.scalar.activation(page[b][:].indirect(L["n5"][:]), dn[b][:], COPY)
             nc.sync.dma_start(out[b * P : (b + 1) * P, :], page[b][:])
 
-        leave_product2(0)
         fetch2(0)
         leave_product2(1)
         fetch2(1)
@@ -277,7 +291,7 @@ def tile_picked_mtthzmhorddpagdd_none_p_kernel(
         put_dn(0)
         put_dn(1)
         for b in (2, 3):
-            open_product2(b)
+            open_product2(b, "o")
             for jh in range(2):
                 close_product2(b, jh)
             leave_product2(b)

from contextlib import ExitStack

import concourse.mybir as mybir
from concourse.masks import make_identity

F32 = mybir.dt.float32
BF16 = mybir.dt.bfloat16
I32 = mybir.dt.int32
U32 = mybir.dt.uint32
U16 = mybir.dt.uint16
U8 = mybir.dt.uint8
FP8X4 = mybir.dt.float8_e4m3fn_x4
ALU = mybir.AluOpType
COPY = mybir.ActivationFunctionType.Copy

P = 128
K, T, S, G, H, W, U = 512, 1024, 256, 2048, 512, 128, 512
PIECE = 256
SPARE = 16
FLOPS = 5 * 2 * K * H * S


def tile_picked_mtthzmhorddpagdd_none_p_kernel(
    tc, x_words, x_scales, d_words, d_scales, gs, offs, k1, two, k2, hz, k3, n1, n2, n3, k4, k5, hy, n4, n5, n6, n7, out
):
    nc = tc.nc
    with ExitStack() as ctx:
        lists = ctx.enter_context(tc.tile_pool(name="lists", bufs=1))
        keep = ctx.enter_context(tc.tile_pool(name="keep", bufs=1))
        psum = ctx.enter_context(tc.psum_pool(name="psum", bufs=2))

        L = {}

        def load_list(name, src):
            L[name] = lists.tile(list(src.shape), U16, name="list_" + name)
            nc.sync.dma_start(L[name][:], src)

        def load_scales(name, src, width):
            t = keep.tile([P, width], U8, name=name)
            rows = src[0].bitcast(I32)
            nc.sync.dma_start(t[:].bitcast(I32), rows.unsqueeze(1).to_broadcast([16, 8, width // 4]))
            return t

        def load_words(name, src, width):
            t = keep.tile([P, width], I32, name=name)
            nc.sync.dma_start(t[:], src[0].rearrange("p n t -> p (n t)").bitcast(I32))
            return t

        x_bytes = load_scales("x_bytes", x_scales, T)
        load_list("offs", offs)
        load_list("two", two)
        load_list("hz", hz)
        d_bytes = load_scales("d_bytes", d_scales, G)
        load_list("k1", k1)
        load_list("k2", k2)
        load_list("k3", k3)
        x_codes = load_words("x_codes", x_words, T)
        d_codes = load_words("d_codes", d_words, G)
        gs_sb = keep.tile([P, 4], F32, name="gs_sb")
        nc.sync.dma_start(gs_sb[:], gs.rearrange("(p t) o -> p (t o)", t=4))
        for name, src in (("n1", n1), ("n2", n2)):
            load_list(name, src)

        ident = keep.tile([P, P], F32, name="ident")
        make_identity(nc, ident[:])

        def offsets(name, piece):
            return L[name][:, piece * PIECE // 16 : (piece + 1) * PIECE // 16]

        scale_of = {}
        words_of = {}

        def gather_bytes(label, picks, after=""):
            width = PIECE * len(picks)
            got = keep.tile([P, width], U8, name="got_" + label, tag=after or "got_" + label, align_bytes=64)
            plane = keep.tile([P, width], U8, name="plane_" + label, align_bytes=64)
            nc.vector.memset(plane[:].bitcast(I32), 0)
            for i, (name, piece) in enumerate(picks):
                table = d_bytes if name.startswith("k") else x_bytes
                nc.vector.tensor_copy(got[:, i * PIECE : (i + 1) * PIECE], table[:].indirect(offsets(name, piece)))
                scale_of[name, piece] = plane[:, i * PIECE : (i + 1) * PIECE]
            for a in range(4):
                nc.sync.dma_start(plane[:].bitcast(I32)[a:P:32, :], got[:].bitcast(I32)[8 * a : P : 32, :])

        def gather_words(name, piece, after=""):
            table = d_codes if name.startswith("k") else x_codes
            got = keep.tile([P, PIECE], U32, name="words_%s_%d" % (name, piece), tag=after or "words_%s_%d" % (name, piece), align_bytes=64)
            nc.vector.tensor_copy(got[:], table[:].bitcast(U32).indirect(offsets(name, piece)))
            words_of[name, piece] = got

        def mx(acc, kname, b, rhs, rhs_scale, start, stop):
            cols = slice((b % 2) * P, (b % 2 + 1) * P)
            nc.tensor.matmul_mx(
                out=acc,
                lhsT=words_of[kname, b // 2][:, cols].bitcast(FP8X4),
                lhsT_scale=scale_of[kname, b // 2][:, cols],
                rhs=rhs.bitcast(FP8X4),
                rhs_scale=rhs_scale,
                start=start,
                stop=stop,
            )

        g_ps = psum.tile([P, 4, P], F32, name="g_ps", tag="back")
        for t in range(4):
            nc.tensor.transpose(g_ps[:, t, :], gs_sb[:, t : t + 1].to_broadcast([P, P]), ident[:])
        gain = keep.tile([P, 2, P, 2], F32, name="gain")
        nc.scalar.activation(gain[:], g_ps[:].rearrange("j (u e) p -> j u p e", e=2), COPY, scale=0.0625)

        h_sb, pa, pb, ra, rb, ub, neg, zt = {}, {}, {}, {}, {}, {}, {}, {}

        def small(name, b):
            return keep.tile([P, W], F32, name="%s%d" % (name, b), tag="%s%d" % (name, b), align_bytes=64)

        def product1(c, terms):
            acc = [psum.tile([P, S], F32, name="h_ps", tag="h") for i in range(2)]
            for n, (kn, xn) in enumerate(terms):
                for i in range(2):
                    mx(acc[i][:], kn, 2 * c + i, words_of[xn, 0][:], scale_of[xn, 0], n == 0, n == 2)
            return acc

        def leave_product1(b, acc, copy):
            h_sb[b] = keep.tile([P, S], F32, name="h%d" % b, tag="h%d" % b)
            copy(h_sb[b][:], acc[:])

        def fetch_pairs(b):
            pa[b] = small("pa", b)
            pb[b] = small("pb", b)
            nc.scalar.activation(pa[b][:], h_sb[b][:].indirect(L["n1"][:]), COPY)
            nc.scalar.activation(pb[b][:], h_sb[b][:].indirect(L["n2"][:]), COPY)

        def order_pairs(b):
            ra[b] = small("ra", b)
            rb[b] = small("rb", b)
            nc.vector.tensor_tensor(ra[b][:], pa[b][:], pb[b][:], ALU.max)
            nc.vector.tensor_tensor(rb[b][:], pa[b][:], pb[b][:], ALU.min)

        def put_larger(b):
            ub[b] = keep.tile([P, S], F32, name="ub%d" % b)
            nc.scalar.activation(ub[b][:].indirect(L["n1"][:]), ra[b][:], COPY)

        def put_smaller(b):
            nc.scalar.activation(ub[b][:].indirect(L["n2"][:]), rb[b][:], COPY)

        def fetch_n3(b, jh, after=""):
            if (b, jh) not in neg:
                neg[b, jh] = keep.tile([P, P], F32, name="neg%d_%d" % (b, jh))
            nc.scalar.activation(neg[b, jh][:], ub[b][:].indirect(L["n3"][:, jh * 8 : (jh + 1) * 8]), COPY, scale=-1.0)

        def turn(blocks, jh, bank):
            cols = slice(jh * P, (jh + 1) * P)
            t1 = psum.tile([P, len(blocks), P], F32, name="t1", tag=bank)
            for i, b in enumerate(blocks):
                nc.tensor.matmul(t1[:, i, :], ub[b][:, cols], ident[:], start=True, stop=False, is_transpose=True)
                nc.tensor.matmul(t1[:, i, :], neg[b, jh][:], ident[:], start=False, stop=True, is_transpose=True)
            ps = slice(32 * blocks[0], 32 * (blocks[-1] + 1))
            nc.vector.tensor_tensor(
                zt[jh][:, :, ps, :], t1[:].rearrange("j b (q u e) -> j u (b q) e", u=2, e=2), gain[:, :, ps, :], ALU.mult
            )

        first = [("offs", 0), ("two", 0), ("hz", 0), ("k1", 0), ("k2", 0), ("k3", 0)]
        gather_bytes("a", first)
        for name, piece in first:
            gather_words(name, piece)
        for name, src in (("n3", n3), ("hy", hy), ("k4", k4), ("k5", k5)):
            load_list(name, src)
        acc = product1(0, (("k1", "offs"), ("k2", "two"), ("k3", "hz")))
        leave_product1(0, acc[0], nc.scalar.copy)
        gather_bytes("b", [("k1", 1), ("k2", 1), ("k3", 1)], "got_a")
        for name, src in (("n6", n6), ("n7", n7), ("n4", n4), ("n5", n5)):
            load_list(name, src)
        fetch_pairs(0)
        leave_product1(1, acc[1], nc.scalar.copy)
        fetch_pairs(1)
        order_pairs(0)
        order_pairs(1)
        gather_words("k3", 1, "pa1")
        gather_words("k1", 1, "pb1")
        put_larger(0)
        put_larger(1)
        gather_words("k2", 1, "ra1")
        put_smaller(0)
        gather_words("hy", 0, "rb0")
        put_smaller(1)
        for jh in range(2):
            fetch_n3(0, jh)
        acc = product1(1, (("k3", "hz"), ("k1", "offs"), ("k2", "two")))
        leave_product1(2, acc[0], nc.vector.tensor_copy)
        leave_product1(3, acc[1], nc.vector.tensor_copy)
        gather_bytes("c", [("hy", 0), ("k5", 0), ("k4", 0)], "ra1")
        fetch_pairs(2)
        fetch_pairs(3)
        late = keep.tile([P, 2, P], F32, name="neg1", tag="h2")
        for jh in range(2):
            neg[1, jh] = late[:, jh, :]
            fetch_n3(1, jh)
        order_pairs(2)
        order_pairs(3)
        gather_words("k5", 0, "pa3")
        gather_words("k4", 0, "pb3")
        put_larger(2)
        put_larger(3)
        put_smaller(2)
        put_smaller(3)
        for jh, after in enumerate(("ra2", "ra3")):
            zt[jh] = keep.tile([P, 2, P, 2], BF16, name="zt%d" % jh, tag=after, align_bytes=64)
            turn((0, 1), jh, "h")
        gather_bytes("d", [("k5", 1), ("k4", 1)], "rb2")
        for jh in range(2):
            fetch_n3(2, jh)
            fetch_n3(3, jh)

        o_ps = {}

        def open_product2(b, bank):
            o_ps[b] = psum.tile([P, S], F32, name="o_ps", tag=bank)
            mx(o_ps[b][:], "k5", b, words_of["hy", 0][:], scale_of["hy", 0], True, False)

        def close_product2(b, jh):
            cols = slice(jh * P, (jh + 1) * P)
            mx(o_ps[b][:, cols], "k4", b, z_codes[:, cols], z_scales[:, cols], False, jh == 1)

        h2 = {}

        def window2(b):
            h2[b] = keep.tile([P, S + SPARE], F32, name="h2_%d" % b)
            nc.gpsimd.memset(h2[b][:, S:], 0.0)

        half = []
        for jh in range(2):
            cols = slice(jh * P, (jh + 1) * P)
            half.append(psum.tile([P, P], F32, name="o_half", tag="o"))
            mx(half[jh][:], "k5", 0, words_of["hy", 0][:, cols], scale_of["hy", 0][:, cols], True, False)
        window2(0)
        z_in = keep.tile([P, S, 4], BF16, name="z_in", align_bytes=64)
        z_codes = keep.tile([P, S], U32, name="z_codes", align_bytes=64)
        z_scales = keep.tile([P, S], U8, name="z_scales", align_bytes=64)
        turn((2, 3), 0, "turn")
        turn((2,), 1, "turn")
        turn((3,), 1, "h")
        open_product2(1, "h")
        for jh in range(2):
            words = zt[jh][:].rearrange("j u p e -> j u (p e)").bitcast(F32)
            t2 = psum.tile([P, 2, P], F32, name="t2", tag="back")
            for u in range(2):
                nc.tensor.transpose(t2[:, u, :], words[:, u, :], ident[:])
            cols = slice(jh * P, (jh + 1) * P)
            nc.scalar.copy(z_in[:, cols, :].bitcast(F32), t2[:].rearrange("p u j -> p j u"))
            nc.vector.quantize_mx(
                out=z_codes[:, cols].bitcast(FP8X4), scales=z_scales[:, cols], in_=z_in[:, cols, :].rearrange("p j t -> p (j t)")
            )
            mx(half[jh][:], "k4", 0, z_codes[:, cols], z_scales[:, cols], False, True)
            nc.vector.tensor_scalar(h2[0][:, cols], half[jh][:], 0.0625, None, ALU.mult)
        for jh in range(2):
            close_product2(1, jh)

        got6, got7, up, dn, page = {}, {}, {}, {}, {}

        def leave_product2(b):
            window2(b)
            nc.vector.tensor_scalar(h2[b][:, :S], o_ps[b][:], 0.0625, None, ALU.mult)

        def fetch2(b):
            got6[b] = keep.tile([P, S], F32, name="got6_%d" % b, tag="got6_%d" % b, align_bytes=64)
            got7[b] = keep.tile([P, S], F32, name="got7_%d" % b, tag="got7_%d" % b, align_bytes=64)
            nc.scalar.activation(got6[b][:], h2[b][:].indirect(L["n6"][:]), COPY)
            nc.scalar.activation(got7[b][:], h2[b][:].indirect(L["n7"][:]), COPY)

        def combine2(b):
            up[b] = keep.tile([P, S], F32, name="up%d" % b)
            dn[b] = keep.tile([P, S], F32, name="dn%d" % b)
            nc.vector.tensor_tensor(up[b][:], h2[b][:, :S], got6[b][:], ALU.max)
            nc.vector.tensor_tensor(dn[b][:], h2[b][:, :S], got7[b][:], ALU.subtract)

        def put_up(b):
            page[b] = keep.tile([P, U], F32, name="page%d" % b)
            nc.scalar.activation(page[b][:].indirect(L["n4"][:]), up[b][:], COPY)

        def put_dn(b):
            nc.scalar.activation(page[b][:].indirect(L["n5"][:]), dn[b][:], COPY)
            nc.sync.dma_start(out[b * P : (b + 1) * P, :], page[b][:])

        fetch2(0)
        leave_product2(1)
        fetch2(1)
        combine2(0)
        gather_words("k5", 1, "got7_0")
        combine2(1)
        gather_words("k4", 1, "got7_1")
        put_up(0)
        put_up(1)
        put_dn(0)
        put_dn(1)
        for b in (2, 3):
            open_product2(b, "o")
            for jh in range(2):
                close_product2(b, jh)
            leave_product2(b)
            fetch2(b)
            combine2(b)
        put_up(2)
        put_up(3)
        put_dn(2)
        put_dn(3)
